import numpy as np
import ml_dtypes


def mxq(x, axis, fmt="e4m3"):
    dtype, down = {"e4m3": (ml_dtypes.float8_e4m3fn, 7), "e5m2": (ml_dtypes.float8_e5m2, 14)}[fmt]
    v = np.moveaxis(np.asarray(x, np.float32).astype(ml_dtypes.bfloat16).astype(np.float64), axis, -1)
    blocks = v.reshape(v.shape[:-1] + (-1, 32))
    amax = np.abs(blocks).max(-1, keepdims=True)
    byte = np.maximum(np.where(amax > 0, np.frexp(amax)[1] - 1 + 127, 0) - down, 1)
    scale = np.exp2(byte - 127.0)
    codes = (blocks / scale).astype(np.float32).astype(dtype).astype(np.float64)
    return np.moveaxis((codes * scale).reshape(v.shape), -1, axis)


WIDE = False


def mx_kscale(k):
    if not WIDE:
        return np.ones(k)
    levels = np.array([10, -10, 5, -5, 0])
    if k % 512:
        return np.exp2(np.random.permutation(np.resize(levels, k // 32))).repeat(32)
    a = np.empty((k // 512, 16))
    for p in range(k // 512):
        a[p, :8] = np.random.permutation(np.resize(levels, 8))
        for g in range(8):
            far = levels[np.abs(levels - a[p, g]) >= 10]
            a[p, g + 8] = far[np.random.randint(len(far))]
    return np.exp2(a.ravel()).repeat(32)


def f64(x):
    return np.asarray(x).astype(np.float64)


def striped(idx):
    return np.tile(idx.reshape(-1, 16).T, (8, 1)).astype(np.uint16)


def unstriped(offs):
    return offs[:16].T.reshape(-1).astype(np.int64)


def pack_weight(w):
    k, n = w.shape
    w = f64(np.asarray(w, np.float32).astype(ml_dtypes.bfloat16)).reshape(k // 32, 32, n)
    amax = np.abs(w).max(1)
    byte = np.clip(np.where(amax > 0, np.frexp(amax)[1] - 1 + 127 - 7, 1), 1, 254)
    scaled = (w * np.exp2(127.0 - byte)[:, None, :]).reshape(k, n).astype(np.float32)
    words = np.ascontiguousarray(scaled.reshape(k // 512, 128, 4, n).transpose(0, 1, 3, 2)).astype(ml_dtypes.float8_e4m3fn).view(np.uint8)
    return words, np.ascontiguousarray(byte.astype(np.uint8).reshape(k // 512, 16, n))


def unpack_weight(words, scales):
    g, p, n, _ = words.shape
    vals = np.ascontiguousarray(words).view(ml_dtypes.float8_e4m3fn).astype(np.float64) * np.repeat(np.exp2(scales.astype(np.float64) - 127.0), 8, axis=1)[..., None]
    return vals.transpose(0, 1, 3, 2).reshape(g * 512, n)


K, T, S, N, H, U = 512, 2048, 512, 128, 512, 1024


def setup_inputs():
    n = np.random.standard_normal
    s = mx_kscale(K)[:, None]
    u = mx_kscale(H)
    packed_xT = pack_weight(n((K, T)) * s)
    return {
        "x_words": packed_xT[0],
        "x_scales": packed_xT[1],
        "w1": (n((K, H)) / np.sqrt(K) / s).astype(np.float32),
        "w2": (n((K, H)) / np.sqrt(K) / s).astype(np.float32),
        "unit": (np.random.uniform(0.6, 1.4, (H, 1)) * u[:, None]).astype(np.float32),
        "w3": (n((H, N)) / np.sqrt(H) / u[:, None]).astype(np.float32),
        "offs": striped(np.random.permutation(T)[:S]),
        "cl1": striped(np.random.permutation(np.concatenate([np.arange(S), np.random.randint(0, S, U - S)]))),
        "exc": striped(np.random.permutation(np.concatenate([np.arange(S), np.random.randint(0, S, U - S)]))),
        "def_": striped(np.random.permutation(np.concatenate([np.arange(S), np.random.randint(0, S, U - S)]))),
    }


def reference(x_words, x_scales, w1, w2, unit, w3, offs, cl1, exc, def_):
    xq = unpack_weight(x_words, x_scales)[:, unstriped(offs)]
    y = mxq(f64(w1), 0, "e4m3").T @ xq
    y_1 = y[:, unstriped(cl1)]
    z1 = mxq(f64(w2), 0, "e4m3").T @ xq
    ze = z1[:, unstriped(exc)]
    yd_ = y[:, unstriped(def_)]
    hid = f64(unit) * (y_1 - (ze * yd_))
    return mxq(f64(w3), 0, "e4m3").T @ mxq(hid, 0, "e4m3")

@@ -1,0 +1,172 @@
+from contextlib import ExitStack
+
+import concourse.mybir as mybir
+
+K, T, S, N, H, U = 512, 2048, 512, 128, 512, 1024
+FLOPS = 2 * K * S * H * 2 + 2 * H * N * U
+
+F32 = mybir.dt.float32
+BF16 = mybir.dt.bfloat16
+I32 = mybir.dt.int32
+U32 = mybir.dt.uint32
+U16 = mybir.dt.uint16
+U8 = mybir.dt.uint8
+FP8X4 = mybir.dt.float8_e4m3fn_x4
+MULT = mybir.AluOpType.mult
+ADD = mybir.AluOpType.add
+COPY = mybir.ActivationFunctionType.Copy
+
+P = 128
+PACK = 4
+CHUNKS = (256, 384, 256, 128)
+FUSED = 1
+
+
+def tile_picked_ywarrnt_exc_p_kernel(tc, x_words, x_scales, w1, w2, unit, w3, offs, cl1, exc, def_, out):
+    nc = tc.nc
+    with ExitStack() as ctx:
+        keep = ctx.enter_context(tc.tile_pool(name="keep", bufs=1))
+        ring = ctx.enter_context(tc.tile_pool(name="ring", bufs=8))
+        wide = ctx.enter_context(tc.tile_pool(name="wide", bufs=3))
+        psum = ctx.enter_context(tc.psum_pool(name="psum", bufs=6))
+        psum_out = ctx.enter_context(tc.psum_pool(name="psum_out", bufs=2))
+
+        offs_sb = keep.tile([P, S // 16], U16, name="offs_sb")
+        cl1_sb = keep.tile([P, U // 16], U16, name="cl1_sb")
+        exc_sb = keep.tile([P, U // 16], U16, name="exc_sb")
+        def_sb = keep.tile([P, U // 16], U16, name="def_sb")
+        x_all = keep.tile([P, T], U32, name="x_all", align_bytes=64)
+        xs_all = keep.tile([P, T], U8, name="xs_all", align_bytes=64)
+        w1_raw = keep.tile([P, PACK, H], F32, name="w1_raw")
+        w2_raw = [keep.tile([P, PACK, H // 2], F32, name=f"w2_raw{h}") for h in range(2)]
+        w3_raw = keep.tile([P, PACK, N], F32, name="w3_raw")
+        unit_sb = keep.tile([P, PACK], F32, name="unit_sb")
+
+        nc.vector.memset(xs_all[:].bitcast(I32), 0)
+        nc.sync.dma_start(out=w1_raw[:], in_=w1.rearrange("(p j) c -> p j c", j=PACK))
+        for q in range(4):
+            nc.sync.dma_start(out=xs_all[32 * q : 32 * q + 4, :].bitcast(I32), in_=x_scales[0, 4 * q : 4 * q + 4, :].bitcast(I32))
+        nc.sync.dma_start(offs_sb[:], offs)
+        nc.sync.dma_start(out=x_all[:].bitcast(I32), in_=x_words[0].rearrange("p n t -> p (n t)").bitcast(I32))
+        nc.sync.dma_start(out=unit_sb[:], in_=unit.rearrange("(p t) o -> p (t o)", t=PACK))
+        for h in range(2):
+            nc.sync.dma_start(out=w2_raw[h][:], in_=w2.rearrange("(p j) c -> p j c", j=PACK)[:, :, h * H // 2 : (h + 1) * H // 2])
+        nc.sync.dma_start(def_sb[:], def_)
+        nc.sync.dma_start(exc_sb[:], exc)
+        nc.sync.dma_start(cl1_sb[:], cl1)
+        nc.sync.dma_start(out=w3_raw[:], in_=w3.rearrange("(p j) c -> p j c", j=PACK))
+
+        w1_bf = keep.tile([P, H * PACK], BF16, name="w1_bf", align_bytes=64)
+        w2_bf = keep.tile([P, H * PACK], BF16, name="w2_bf", align_bytes=64)
+        w3_bf = keep.tile([P, N * PACK], BF16, name="w3_bf", align_bytes=64)
+        w1_codes = keep.tile([P, H], U32, name="w1_codes", align_bytes=64)
+        w2_codes = keep.tile([P, H], U32, name="w2_codes", align_bytes=64)
+        w3_codes = keep.tile([P, N], U32, name="w3_codes", align_bytes=64)
+        w1_scales = keep.tile([P, H], U8, name="w1_scales", align_bytes=64)
+        w2_scales = keep.tile([P, H], U8, name="w2_scales", align_bytes=64)
+        w3_scales = keep.tile([P, N], U8, name="w3_scales", align_bytes=64)
+
+        def dealt(bf, m0, m1, raw):
+            dst = bf[:].rearrange("p (t m j) -> p m j t", t=PACK, j=PACK)[:, m0:m1]
+            return dst, raw.rearrange("p j (m t) -> p m j t", t=PACK)
+
+        def quantize(codes, scales, bf, c0, c1):
+            nc.vector.quantize_mx(out=codes[:, c0:c1].bitcast(FP8X4), scales=scales[:, c0:c1], in_=bf[:, PACK * c0 : PACK * c1])
+
+        x_codes = keep.tile([P, S], U32, name="x_codes", align_bytes=64)
+        x_bytes = keep.tile([P, S], U8, name="x_bytes", align_bytes=64)
+
+        nc.scalar.copy(*dealt(w1_bf, 0, 64, w1_raw[:, :, : H // 2]))
+        nc.vector.tensor_copy(*dealt(w1_bf, 64, 128, w1_raw[:, :, H // 2 :]))
+        nc.vector.tensor_copy(x_bytes[:], xs_all[:].indirect(offs_sb[:]))
+        quantize(w1_codes, w1_scales, w1_bf, 0, H)
+        nc.vector.tensor_copy(x_codes[:], x_all[:].indirect(offs_sb[:]))
+
+        def project(codes, scales, t):
+            acc = psum.tile([P, S], F32, name="acc")
+            cols = slice(t * P, (t + 1) * P)
+            nc.tensor.matmul_mx(out=acc[:], lhsT=codes[:, cols].bitcast(FP8X4), lhsT_scale=scales[:, cols],
+                                rhs=x_codes[:].bitcast(FP8X4), rhs_scale=x_bytes[:], start=True, stop=True)
+            return acc
+
+        y = [keep.tile([P, S], F32, name=f"y{t}") for t in range(PACK)]
+        z = [keep.tile([P, S], F32, name=f"z{t}") for t in range(PACK)]
+        starts = [sum(CHUNKS[:c]) for c in range(len(CHUNKS))]
+
+        def entries(c):
+            return slice(starts[c] // 16, (starts[c] + CHUNKS[c]) // 16)
+
+        def definition(c, t):
+            yd = ring.tile([P, CHUNKS[c]], F32, name="yd")
+            nc.scalar.activation(yd[:], y[t][:].indirect(def_sb[:, entries(c)]), COPY)
+            return yd
+
+        def paired(tile):
+            return tile[:].rearrange("p t (c i) -> p c t i", i=2)
+
+        def woven(tile):
+            return tile[:].rearrange("p (c i t) -> p c t i", i=2, t=PACK)
+
+        def fused_chunk(c, yds):
+            n = CHUNKS[c]
+            hid = wide.tile([P, PACK, n], F32, name="hid")
+            prods = [ring.tile([P, n], F32, name="prod") for t in range(PACK)]
+            for step in range(PACK + 1):
+                if step < PACK:
+                    nc.vector.tensor_tensor(prods[step][:], z[step][:].indirect(exc_sb[:, entries(c)]), yds[step][:], MULT)
+                if step >= 1:
+                    t = step - 1
+                    nc.vector.tensor_tensor(hid[:, t, :], y[t][:].indirect(cl1_sb[:, entries(c)]), prods[t][:], ADD)
+            hid_bf = wide.tile([P, n * PACK], BF16, name="hid_bf", align_bytes=64)
+            nc.vector.tensor_copy(woven(hid_bf), paired(hid))
+            return hid_bf
+
+        def split_chunk(c, yds):
+            n = CHUNKS[c]
+            clause = wide.tile([P, PACK, n], F32, name="clause")
+            lost = wide.tile([P, PACK, n], F32, name="lost")
+            for t in range(PACK):
+                nc.scalar.activation(clause[:, t, :], y[t][:].indirect(cl1_sb[:, entries(c)]), COPY)
+            for t in range(PACK):
+                nc.vector.tensor_tensor(lost[:, t, :], z[t][:].indirect(exc_sb[:, entries(c)]), yds[t][:], MULT)
+            hid_bf = wide.tile([P, n * PACK], BF16, name="hid_bf", align_bytes=64)
+            nc.vector.tensor_tensor(woven(hid_bf), paired(clause), paired(lost), ADD)
+            return hid_bf
+
+        def finish(c, hid_bf):
+            n = CHUNKS[c]
+            hid_codes = wide.tile([P, n], U32, name="hid_codes", align_bytes=64)
+            hid_scales = wide.tile([P, n], U8, name="hid_scales", align_bytes=64)
+            quantize(hid_codes, hid_scales, hid_bf, 0, n)
+            acc = psum_out.tile([P, n], F32, name="acc_out")
+            for c0 in range(0, n, 256):
+                c1 = min(c0 + 256, n)
+                nc.tensor.matmul_mx(out=acc[:, c0:c1], lhsT=w3_codes[:].bitcast(FP8X4), lhsT_scale=w3_scales[:],
+                                    rhs=hid_codes[:, c0:c1].bitcast(FP8X4), rhs_scale=hid_scales[:, c0:c1], start=True, stop=True)
+            res = wide.tile([P, n], F32, name="res")
+            nc.vector.tensor_copy(res[:], acc[:])
+            nc.sync.dma_start(out=out[:, starts[c] : starts[c] + n], in_=res[:])
+
+        y_acc = [project(w1_codes, w1_scales, t) for t in range(PACK)]
+        for h in range(2):
+            nc.vector.tensor_copy(*dealt(w2_bf, 64 * h, 64 * (h + 1), w2_raw[h][:]))
+        quantize(w2_codes, w2_scales, w2_bf, 0, P)
+        quantize(w2_codes, w2_scales, w2_bf, P, H)
+        yds = []
+        for t in range(PACK):
+            nc.scalar.activation(y[t][:], y_acc[t][:], COPY, scale=unit_sb[:, t : t + 1])
+            yds.append(definition(0, t))
+            acc = project(w2_codes, w2_scales, t)
+            if t < 1:
+                nc.vector.tensor_scalar(z[t][:], acc[:], -1.0, None, MULT)
+            else:
+                nc.scalar.activation(z[t][:], acc[:], COPY, scale=-1.0)
+
+        nc.vector.tensor_copy(w3_bf[:].rearrange("p (c j) -> p c j", j=PACK), w3_raw[:].rearrange("p j c -> p c j"))
+        quantize(w3_codes, w3_scales, w3_bf, 0, N)
+
+        for c in range(len(CHUNKS)):
+            hid_bf = fused_chunk(c, yds) if c < FUSED else split_chunk(c, yds)
+            if c + 1 < len(CHUNKS):
+                yds = [definition(c + 1, t) for t in range(PACK)]
+            finish(c, hid_bf)

@@ -18,18 +18,23 @@ COPY = mybir.ActivationFunctionType.Copy
 
 P = 128
 PACK = 4
-CHUNKS = (256, 384, 256, 128)
-FUSED = 1
+SPARE = 528
+CHUNKS = (256, 256, 256, 128, 128)
+PIECES = (1024,)
+FIRST = (1024,)
+Y_ON_VECTOR = ()
+Z_ON_VECTOR = (0, 1, 2, 3)
+CLAUSE_ON_VECTOR = (2, 0, 0, 0, 0)
+OUT_ON_SCALAR = (0, 1, 2, 3, 4)
 
 
 def tile_picked_ywarrnt_exc_p_kernel(tc, x_words, x_scales, w1, w2, unit, w3, offs, cl1, exc, def_, out):
     nc = tc.nc
     with ExitStack() as ctx:
         keep = ctx.enter_context(tc.tile_pool(name="keep", bufs=1))
-        ring = ctx.enter_context(tc.tile_pool(name="ring", bufs=8))
-        wide = ctx.enter_context(tc.tile_pool(name="wide", bufs=3))
-        psum = ctx.enter_context(tc.psum_pool(name="psum", bufs=6))
-        psum_out = ctx.enter_context(tc.psum_pool(name="psum_out", bufs=2))
+        ring = ctx.enter_context(tc.tile_pool(name="ring", bufs=5))
+        wide = ctx.enter_context(tc.tile_pool(name="wide", bufs=5))
+        psum = ctx.enter_context(tc.psum_pool(name="psum", bufs=8))
 
         offs_sb = keep.tile([P, S // 16], U16, name="offs_sb")
         cl1_sb = keep.tile([P, U // 16], U16, name="cl1_sb")
@@ -44,8 +49,8 @@ def tile_picked_ywarrnt_exc_p_kernel(tc, x_words, x_scales, w1, w2, unit, w3, of
 
         nc.vector.memset(xs_all[:].bitcast(I32), 0)
         nc.sync.dma_start(out=w1_raw[:], in_=w1.rearrange("(p j) c -> p j c", j=PACK))
-        for q in range(4):
-            nc.sync.dma_start(out=xs_all[32 * q : 32 * q + 4, :].bitcast(I32), in_=x_scales[0, 4 * q : 4 * q + 4, :].bitcast(I32))
+        for r in range(4):
+            nc.sync.dma_start(out=xs_all[r:P:32, :].bitcast(I32), in_=x_scales[0, r:16:4, :].bitcast(I32))
         nc.sync.dma_start(offs_sb[:], offs)
         nc.sync.dma_start(out=x_all[:].bitcast(I32), in_=x_words[0].rearrange("p n t -> p (n t)").bitcast(I32))
         nc.sync.dma_start(out=unit_sb[:], in_=unit.rearrange("(p t) o -> p (t o)", t=PACK))
@@ -80,93 +85,74 @@ def tile_picked_ywarrnt_exc_p_kernel(tc, x_words, x_scales, w1, w2, unit, w3, of
         nc.vector.tensor_copy(*dealt(w1_bf, 64, 128, w1_raw[:, :, H // 2 :]))
         nc.vector.tensor_copy(x_bytes[:], xs_all[:].indirect(offs_sb[:]))
         quantize(w1_codes, w1_scales, w1_bf, 0, H)
-        nc.vector.tensor_copy(x_codes[:], x_all[:].indirect(offs_sb[:]))
+        for h in range(2):
+            nc.vector.tensor_copy(x_codes[:, h * S // 2 : (h + 1) * S // 2], x_all[:].indirect(offs_sb[:, h * S // 32 : (h + 1) * S // 32]))
 
-        def project(codes, scales, t):
-            acc = psum.tile([P, S], F32, name="acc")
+        def project(codes, scales, t, j0=0, j1=S):
+            acc = psum.tile([P, j1 - j0], F32, name="acc")
             cols = slice(t * P, (t + 1) * P)
             nc.tensor.matmul_mx(out=acc[:], lhsT=codes[:, cols].bitcast(FP8X4), lhsT_scale=scales[:, cols],
-                                rhs=x_codes[:].bitcast(FP8X4), rhs_scale=x_bytes[:], start=True, stop=True)
+                                rhs=x_codes[:, j0:j1].bitcast(FP8X4), rhs_scale=x_bytes[:, j0:j1], start=True, stop=True)
             return acc
 
-        y = [keep.tile([P, S], F32, name=f"y{t}") for t in range(PACK)]
-        z = [keep.tile([P, S], F32, name=f"z{t}") for t in range(PACK)]
-        starts = [sum(CHUNKS[:c]) for c in range(len(CHUNKS))]
-
-        def entries(c):
-            return slice(starts[c] // 16, (starts[c] + CHUNKS[c]) // 16)
-
-        def definition(c, t):
-            yd = ring.tile([P, CHUNKS[c]], F32, name="yd")
-            nc.scalar.activation(yd[:], y[t][:].indirect(def_sb[:, entries(c)]), COPY)
-            return yd
-
-        def paired(tile):
-            return tile[:].rearrange("p t (c i) -> p c t i", i=2)
+        y = [keep.tile([P, S + SPARE], F32, name=f"y{t}") for t in range(PACK)]
+        z = [keep.tile([P, S + SPARE], F32, name=f"z{t}") for t in range(PACK)]
+        def paired(ap):
+            return ap.rearrange("p t (c i) -> p c t i", i=2)
 
         def woven(tile):
             return tile[:].rearrange("p (c i t) -> p c t i", i=2, t=PACK)
 
-        def fused_chunk(c, yds):
-            n = CHUNKS[c]
-            hid = wide.tile([P, PACK, n], F32, name="hid")
-            prods = [ring.tile([P, n], F32, name="prod") for t in range(PACK)]
-            for step in range(PACK + 1):
-                if step < PACK:
-                    nc.vector.tensor_tensor(prods[step][:], z[step][:].indirect(exc_sb[:, entries(c)]), yds[step][:], MULT)
-                if step >= 1:
-                    t = step - 1
-                    nc.vector.tensor_tensor(hid[:, t, :], y[t][:].indirect(cl1_sb[:, entries(c)]), prods[t][:], ADD)
-            hid_bf = wide.tile([P, n * PACK], BF16, name="hid_bf", align_bytes=64)
-            nc.vector.tensor_copy(woven(hid_bf), paired(hid))
-            return hid_bf
-
-        def split_chunk(c, yds):
-            n = CHUNKS[c]
-            clause = wide.tile([P, PACK, n], F32, name="clause")
-            lost = wide.tile([P, PACK, n], F32, name="lost")
-            for t in range(PACK):
-                nc.scalar.activation(clause[:, t, :], y[t][:].indirect(cl1_sb[:, entries(c)]), COPY)
-            for t in range(PACK):
-                nc.vector.tensor_tensor(lost[:, t, :], z[t][:].indirect(exc_sb[:, entries(c)]), yds[t][:], MULT)
-            hid_bf = wide.tile([P, n * PACK], BF16, name="hid_bf", align_bytes=64)
-            nc.vector.tensor_tensor(woven(hid_bf), paired(clause), paired(lost), ADD)
-            return hid_bf
-
-        def finish(c, hid_bf):
-            n = CHUNKS[c]
-            hid_codes = wide.tile([P, n], U32, name="hid_codes", align_bytes=64)
-            hid_scales = wide.tile([P, n], U8, name="hid_scales", align_bytes=64)
-            quantize(hid_codes, hid_scales, hid_bf, 0, n)
-            acc = psum_out.tile([P, n], F32, name="acc_out")
-            for c0 in range(0, n, 256):
-                c1 = min(c0 + 256, n)
-                nc.tensor.matmul_mx(out=acc[:, c0:c1], lhsT=w3_codes[:].bitcast(FP8X4), lhsT_scale=w3_scales[:],
-                                    rhs=hid_codes[:, c0:c1].bitcast(FP8X4), rhs_scale=hid_scales[:, c0:c1], start=True, stop=True)
-            res = wide.tile([P, n], F32, name="res")
-            nc.vector.tensor_copy(res[:], acc[:])
-            nc.sync.dma_start(out=out[:, starts[c] : starts[c] + n], in_=res[:])
-
-        y_acc = [project(w1_codes, w1_scales, t) for t in range(PACK)]
-        for h in range(2):
-            nc.vector.tensor_copy(*dealt(w2_bf, 64 * h, 64 * (h + 1), w2_raw[h][:]))
-        quantize(w2_codes, w2_scales, w2_bf, 0, P)
-        quantize(w2_codes, w2_scales, w2_bf, P, H)
-        yds = []
-        for t in range(PACK):
-            nc.scalar.activation(y[t][:], y_acc[t][:], COPY, scale=unit_sb[:, t : t + 1])
-            yds.append(definition(0, t))
-            acc = project(w2_codes, w2_scales, t)
-            if t < 1:
-                nc.vector.tensor_scalar(z[t][:], acc[:], -1.0, None, MULT)
+        def leave(dst, acc, scale, on_vector):
+            if on_vector:
+                nc.vector.tensor_scalar(dst, acc[:], scale, None, MULT)
             else:
-                nc.scalar.activation(z[t][:], acc[:], COPY, scale=-1.0)
+                nc.scalar.activation(dst, acc[:], COPY, scale=scale)
 
-        nc.vector.tensor_copy(w3_bf[:].rearrange("p (c j) -> p c j", j=PACK), w3_raw[:].rearrange("p j c -> p c j"))
+        early = project(w1_codes, w1_scales, 0, 0, S // 2)
+        leave(y[0][:, : S // 2], early, unit_sb[:, 0:1], False)
+        y_from = [S // 2, 0, 0, 0]
+        y_acc = [project(w1_codes, w1_scales, t, y_from[t]) for t in range(PACK)]
+        nc.vector.tensor_copy(*dealt(w2_bf, 0, 64, w2_raw[0][:]))
+        nc.vector.tensor_copy(*dealt(w2_bf, 64, 128, w2_raw[1][:]))
+        quantize(w2_codes, w2_scales, w2_bf, 0, H)
+        defined = keep.tile([P, PACK, U], F32, name="defined")
+        lost = keep.tile([P, PACK, U], F32, name="lost")
+        for t in range(PACK):
+            leave(y[t][:, y_from[t] : S], y_acc[t], unit_sb[:, t : t + 1], t in Y_ON_VECTOR)
+            pieces = FIRST if t == 0 else PIECES
+            spans = [(sum(pieces[:i]), sum(pieces[: i + 1])) for i in range(len(pieces))]
+            for r0, r1 in spans:
+                nc.scalar.activation(defined[:, t, r0:r1], y[t][:].indirect(def_sb[:, r0 // 16 : r1 // 16]), COPY)
+            leave(z[t][:, :S], project(w2_codes, w2_scales, t), -1.0, t in Z_ON_VECTOR)
+            for r0, r1 in spans:
+                nc.vector.tensor_tensor(lost[:, t, r0:r1], z[t][:].indirect(exc_sb[:, r0 // 16 : r1 // 16]), defined[:, t, r0:r1], MULT)
+
+        nc.vector.tensor_copy(*(w3_bf[:].rearrange("p (c j) -> p c j", j=PACK), w3_raw[:].rearrange("p j c -> p c j")))
         quantize(w3_codes, w3_scales, w3_bf, 0, N)
 
-        for c in range(len(CHUNKS)):
-            hid_bf = fused_chunk(c, yds) if c < FUSED else split_chunk(c, yds)
-            if c + 1 < len(CHUNKS):
-                yds = [definition(c + 1, t) for t in range(PACK)]
-            finish(c, hid_bf)
+        r0 = 0
+        for c, n in enumerate(CHUNKS):
+            clause = wide.tile([P, PACK, n], F32, name="clause")
+            for t in range(PACK):
+                found = y[t][:].indirect(cl1_sb[:, r0 // 16 : (r0 + n) // 16])
+                if t >= PACK - CLAUSE_ON_VECTOR[c]:
+                    nc.vector.tensor_copy(clause[:, t, :], found)
+                else:
+                    nc.scalar.activation(clause[:, t, :], found, COPY)
+            hid_bf = ring.tile([P, n * PACK], BF16, name="hid_bf", align_bytes=64)
+            nc.vector.tensor_tensor(woven(hid_bf), paired(clause[:]), paired(lost[:, :, r0 : r0 + n]), ADD)
+            hid_codes = ring.tile([P, n], U32, name="hid_codes", align_bytes=64)
+            hid_scales = ring.tile([P, n], U8, name="hid_scales", align_bytes=64)
+            quantize(hid_codes, hid_scales, hid_bf, 0, n)
+            acc = psum.tile([P, n], F32, name="acc")
+            for c0, c1 in ([(0, 256), (256, n)] if n == 384 else [(0, n)]):
+                nc.tensor.matmul_mx(out=acc[:, c0:c1], lhsT=w3_codes[:].bitcast(FP8X4), lhsT_scale=w3_scales[:],
+                                    rhs=hid_codes[:, c0:c1].bitcast(FP8X4), rhs_scale=hid_scales[:, c0:c1], start=True, stop=True)
+            res = ring.tile([P, n], F32, name="res")
+            if c in OUT_ON_SCALAR:
+                nc.scalar.copy(res[:], acc[:])
+            else:
+                nc.vector.tensor_copy(res[:], acc[:])
+            nc.sync.dma_start(out=out[:, r0 : r0 + n], in_=res[:])
+            r0 += n

@@ -98,10 +98,10 @@ def tile_picked_ywarrnt_exc_p_kernel(tc, x_words, x_scales, w1, w2, unit, w3, of
         y = [keep.tile([P, S + SPARE], F32, name=f"y{t}") for t in range(PACK)]
         z = [keep.tile([P, S + SPARE], F32, name=f"z{t}") for t in range(PACK)]
         def paired(ap):
-            return ap.rearrange("p t (c i) -> p c t i", i=2)
+            return ap.rearrange("p t (c i) -> p c t i", i=4)
 
         def woven(tile):
-            return tile[:].rearrange("p (c i t) -> p c t i", i=2, t=PACK)
+            return tile[:].rearrange("p (c i t) -> p c t i", i=4, t=PACK)
 
         def leave(dst, acc, scale, on_vector):
             if on_vector:

from contextlib import ExitStack

import concourse.mybir as mybir

K, T, S, N, H, U = 512, 2048, 512, 128, 512, 1024
FLOPS = 2 * K * S * H * 2 + 2 * H * N * U

F32 = mybir.dt.float32
BF16 = mybir.dt.bfloat16
I32 = mybir.dt.int32
U32 = mybir.dt.uint32
U16 = mybir.dt.uint16
U8 = mybir.dt.uint8
FP8X4 = mybir.dt.float8_e4m3fn_x4
MULT = mybir.AluOpType.mult
ADD = mybir.AluOpType.add
COPY = mybir.ActivationFunctionType.Copy

P = 128
PACK = 4
SPARE = 528
CHUNKS = (256, 256, 256, 128, 128)
PIECES = (1024,)
FIRST = (1024,)
Y_ON_VECTOR = ()
Z_ON_VECTOR = (0, 1, 2, 3)
CLAUSE_ON_VECTOR = (2, 0, 0, 0, 0)
OUT_ON_SCALAR = (0, 1, 2, 3, 4)


def tile_picked_ywarrnt_exc_p_kernel(tc, x_words, x_scales, w1, w2, unit, w3, offs, cl1, exc, def_, out):
    nc = tc.nc
    with ExitStack() as ctx:
        keep = ctx.enter_context(tc.tile_pool(name="keep", bufs=1))
        ring = ctx.enter_context(tc.tile_pool(name="ring", bufs=5))
        wide = ctx.enter_context(tc.tile_pool(name="wide", bufs=5))
        psum = ctx.enter_context(tc.psum_pool(name="psum", bufs=8))

        offs_sb = keep.tile([P, S // 16], U16, name="offs_sb")
        cl1_sb = keep.tile([P, U // 16], U16, name="cl1_sb")
        exc_sb = keep.tile([P, U // 16], U16, name="exc_sb")
        def_sb = keep.tile([P, U // 16], U16, name="def_sb")
        x_all = keep.tile([P, T], U32, name="x_all", align_bytes=64)
        xs_all = keep.tile([P, T], U8, name="xs_all", align_bytes=64)
        w1_raw = keep.tile([P, PACK, H], F32, name="w1_raw")
        w2_raw = [keep.tile([P, PACK, H // 2], F32, name=f"w2_raw{h}") for h in range(2)]
        w3_raw = keep.tile([P, PACK, N], F32, name="w3_raw")
        unit_sb = keep.tile([P, PACK], F32, name="unit_sb")

        nc.vector.memset(xs_all[:].bitcast(I32), 0)
        nc.sync.dma_start(out=w1_raw[:], in_=w1.rearrange("(p j) c -> p j c", j=PACK))
        for r in range(4):
            nc.sync.dma_start(out=xs_all[r:P:32, :].bitcast(I32), in_=x_scales[0, r:16:4, :].bitcast(I32))
        nc.sync.dma_start(offs_sb[:], offs)
        nc.sync.dma_start(out=x_all[:].bitcast(I32), in_=x_words[0].rearrange("p n t -> p (n t)").bitcast(I32))
        nc.sync.dma_start(out=unit_sb[:], in_=unit.rearrange("(p t) o -> p (t o)", t=PACK))
        for h in range(2):
            nc.sync.dma_start(out=w2_raw[h][:], in_=w2.rearrange("(p j) c -> p j c", j=PACK)[:, :, h * H // 2 : (h + 1) * H // 2])
        nc.sync.dma_start(def_sb[:], def_)
        nc.sync.dma_start(exc_sb[:], exc)
        nc.sync.dma_start(cl1_sb[:], cl1)
        nc.sync.dma_start(out=w3_raw[:], in_=w3.rearrange("(p j) c -> p j c", j=PACK))

        w1_bf = keep.tile([P, H * PACK], BF16, name="w1_bf", align_bytes=64)
        w2_bf = keep.tile([P, H * PACK], BF16, name="w2_bf", align_bytes=64)
        w3_bf = keep.tile([P, N * PACK], BF16, name="w3_bf", align_bytes=64)
        w1_codes = keep.tile([P, H], U32, name="w1_codes", align_bytes=64)
        w2_codes = keep.tile([P, H], U32, name="w2_codes", align_bytes=64)
        w3_codes = keep.tile([P, N], U32, name="w3_codes", align_bytes=64)
        w1_scales = keep.tile([P, H], U8, name="w1_scales", align_bytes=64)
        w2_scales = keep.tile([P, H], U8, name="w2_scales", align_bytes=64)
        w3_scales = keep.tile([P, N], U8, name="w3_scales", align_bytes=64)

        def dealt(bf, m0, m1, raw):
            dst = bf[:].rearrange("p (t m j) -> p m j t", t=PACK, j=PACK)[:, m0:m1]
            return dst, raw.rearrange("p j (m t) -> p m j t", t=PACK)

        def quantize(codes, scales, bf, c0, c1):
            nc.vector.quantize_mx(out=codes[:, c0:c1].bitcast(FP8X4), scales=scales[:, c0:c1], in_=bf[:, PACK * c0 : PACK * c1])

        x_codes = keep.tile([P, S], U32, name="x_codes", align_bytes=64)
        x_bytes = keep.tile([P, S], U8, name="x_bytes", align_bytes=64)

        nc.scalar.copy(*dealt(w1_bf, 0, 64, w1_raw[:, :, : H // 2]))
        nc.vector.tensor_copy(*dealt(w1_bf, 64, 128, w1_raw[:, :, H // 2 :]))
        nc.vector.tensor_copy(x_bytes[:], xs_all[:].indirect(offs_sb[:]))
        quantize(w1_codes, w1_scales, w1_bf, 0, H)
        for h in range(2):
            nc.vector.tensor_copy(x_codes[:, h * S // 2 : (h + 1) * S // 2], x_all[:].indirect(offs_sb[:, h * S // 32 : (h + 1) * S // 32]))

        def project(codes, scales, t, j0=0, j1=S):
            acc = psum.tile([P, j1 - j0], F32, name="acc")
            cols = slice(t * P, (t + 1) * P)
            nc.tensor.matmul_mx(out=acc[:], lhsT=codes[:, cols].bitcast(FP8X4), lhsT_scale=scales[:, cols],
                                rhs=x_codes[:, j0:j1].bitcast(FP8X4), rhs_scale=x_bytes[:, j0:j1], start=True, stop=True)
            return acc

        y = [keep.tile([P, S + SPARE], F32, name=f"y{t}") for t in range(PACK)]
        z = [keep.tile([P, S + SPARE], F32, name=f"z{t}") for t in range(PACK)]
        def paired(ap):
            return ap.rearrange("p t (c i) -> p c t i", i=4)

        def woven(tile):
            return tile[:].rearrange("p (c i t) -> p c t i", i=4, t=PACK)

        def leave(dst, acc, scale, on_vector):
            if on_vector:
                nc.vector.tensor_scalar(dst, acc[:], scale, None, MULT)
            else:
                nc.scalar.activation(dst, acc[:], COPY, scale=scale)

        early = project(w1_codes, w1_scales, 0, 0, S // 2)
        leave(y[0][:, : S // 2], early, unit_sb[:, 0:1], False)
        y_from = [S // 2, 0, 0, 0]
        y_acc = [project(w1_codes, w1_scales, t, y_from[t]) for t in range(PACK)]
        nc.vector.tensor_copy(*dealt(w2_bf, 0, 64, w2_raw[0][:]))
        nc.vector.tensor_copy(*dealt(w2_bf, 64, 128, w2_raw[1][:]))
        quantize(w2_codes, w2_scales, w2_bf, 0, H)
        defined = keep.tile([P, PACK, U], F32, name="defined")
        lost = keep.tile([P, PACK, U], F32, name="lost")
        for t in range(PACK):
            leave(y[t][:, y_from[t] : S], y_acc[t], unit_sb[:, t : t + 1], t in Y_ON_VECTOR)
            pieces = FIRST if t == 0 else PIECES
            spans = [(sum(pieces[:i]), sum(pieces[: i + 1])) for i in range(len(pieces))]
            for r0, r1 in spans:
                nc.scalar.activation(defined[:, t, r0:r1], y[t][:].indirect(def_sb[:, r0 // 16 : r1 // 16]), COPY)
            leave(z[t][:, :S], project(w2_codes, w2_scales, t), -1.0, t in Z_ON_VECTOR)
            for r0, r1 in spans:
                nc.vector.tensor_tensor(lost[:, t, r0:r1], z[t][:].indirect(exc_sb[:, r0 // 16 : r1 // 16]), defined[:, t, r0:r1], MULT)

        nc.vector.tensor_copy(*(w3_bf[:].rearrange("p (c j) -> p c j", j=PACK), w3_raw[:].rearrange("p j c -> p c j")))
        quantize(w3_codes, w3_scales, w3_bf, 0, N)

        r0 = 0
        for c, n in enumerate(CHUNKS):
            clause = wide.tile([P, PACK, n], F32, name="clause")
            for t in range(PACK):
                found = y[t][:].indirect(cl1_sb[:, r0 // 16 : (r0 + n) // 16])
                if t >= PACK - CLAUSE_ON_VECTOR[c]:
                    nc.vector.tensor_copy(clause[:, t, :], found)
                else:
                    nc.scalar.activation(clause[:, t, :], found, COPY)
            hid_bf = ring.tile([P, n * PACK], BF16, name="hid_bf", align_bytes=64)
            nc.vector.tensor_tensor(woven(hid_bf), paired(clause[:]), paired(lost[:, :, r0 : r0 + n]), ADD)
            hid_codes = ring.tile([P, n], U32, name="hid_codes", align_bytes=64)
            hid_scales = ring.tile([P, n], U8, name="hid_scales", align_bytes=64)
            quantize(hid_codes, hid_scales, hid_bf, 0, n)
            acc = psum.tile([P, n], F32, name="acc")
            for c0, c1 in ([(0, 256), (256, n)] if n == 384 else [(0, n)]):
                nc.tensor.matmul_mx(out=acc[:, c0:c1], lhsT=w3_codes[:].bitcast(FP8X4), lhsT_scale=w3_scales[:],
                                    rhs=hid_codes[:, c0:c1].bitcast(FP8X4), rhs_scale=hid_scales[:, c0:c1], start=True, stop=True)
            res = ring.tile([P, n], F32, name="res")
            if c in OUT_ON_SCALAR:
                nc.scalar.copy(res[:], acc[:])
            else:
                nc.vector.tensor_copy(res[:], acc[:])
            nc.sync.dma_start(out=out[:, r0 : r0 + n], in_=res[:])
            r0 += n
